import numpy as np
import ml_dtypes


def mxq(x, axis, fmt="e4m3"):
    dtype, down = {"e4m3": (ml_dtypes.float8_e4m3fn, 7), "e5m2": (ml_dtypes.float8_e5m2, 14)}[fmt]
    v = np.moveaxis(np.asarray(x, np.float32).astype(ml_dtypes.bfloat16).astype(np.float64), axis, -1)
    blocks = v.reshape(v.shape[:-1] + (-1, 32))
    amax = np.abs(blocks).max(-1, keepdims=True)
    byte = np.maximum(np.where(amax > 0, np.frexp(amax)[1] - 1 + 127, 0) - down, 1)
    scale = np.exp2(byte - 127.0)
    codes = (blocks / scale).astype(np.float32).astype(dtype).astype(np.float64)
    return np.moveaxis((codes * scale).reshape(v.shape), -1, axis)


WIDE = False


def mx_kscale(k):
    if not WIDE:
        return np.ones(k)
    levels = np.array([10, -10, 5, -5, 0])
    if k % 512:
        return np.exp2(np.random.permutation(np.resize(levels, k // 32))).repeat(32)
    a = np.empty((k // 512, 16))
    for p in range(k // 512):
        a[p, :8] = np.random.permutation(np.resize(levels, 8))
        for g in range(8):
            far = levels[np.abs(levels - a[p, g]) >= 10]
            a[p, g + 8] = far[np.random.randint(len(far))]
    return np.exp2(a.ravel()).repeat(32)


def f64(x):
    return np.asarray(x).astype(np.float64)


def striped8(idx):
    return np.asarray(idx).reshape(8, -1, 16).transpose(0, 2, 1).reshape(128, -1).astype(np.uint16)


def unstriped8(offs):
    return offs.reshape(8, 16, -1).transpose(0, 2, 1).reshape(8, -1).astype(np.int64)


def pick8(x, idx, run):
    r = np.arange(len(x))
    return x[r[:, None], idx[r % (8 * run) // run]]


E2M1 = np.array([0.0, 0.5, 1.0, 1.5, 2.0, 3.0, 4.0, 6.0, -0.0, -0.5, -1.0, -1.5, -2.0, -3.0, -4.0, -6.0])


def pack_weight(w, fmt):
    k, n = w.shape
    w = f64(np.asarray(w, np.float32).astype(ml_dtypes.bfloat16)).reshape(k // 32, 32, n)
    amax = np.abs(w).max(1)
    if fmt == "e4m3":
        byte = np.frexp(amax)[1] - 1 + 127 - 7
    else:
        mant, ex = np.frexp(amax / 6.0)
        byte = np.where(mant > 0.5, ex, ex - 1) + 127
    byte = np.clip(np.where(amax > 0, byte, 1), 1, 254)
    scaled = (w * np.exp2(127.0 - byte)[:, None, :]).reshape(k, n).astype(np.float32)
    by_word = np.ascontiguousarray(scaled.reshape(k // 512, 128, 4, n).transpose(0, 1, 3, 2))
    if fmt == "e4m3":
        words = by_word.astype(ml_dtypes.float8_e4m3fn).view(np.uint8)
    else:
        c = by_word.astype(ml_dtypes.float4_e2m1fn).view(np.uint8) & 0xF
        words = (c[..., 0::2] | (c[..., 1::2] << 4)).reshape(k // 512, 128, 2 * n)
    return np.ascontiguousarray(words), np.ascontiguousarray(byte.astype(np.uint8).reshape(k // 512, 16, n))


def unpack_weight(words, scales, fmt):
    g, _, n = scales.shape
    words = np.ascontiguousarray(words).reshape(g, 128, n, -1)
    if fmt == "e4m3":
        vals = words.view(ml_dtypes.float8_e4m3fn).astype(np.float64)
    else:
        nib = np.empty((g, 128, n, 4), np.uint8)
        nib[..., 0::2] = words & 0xF
        nib[..., 1::2] = words >> 4
        vals = E2M1[nib]
    vals = vals * np.repeat(np.exp2(scales.astype(np.float64) - 127.0), 8, axis=1)[..., None]
    return vals.transpose(0, 1, 3, 2).reshape(g * 512, n)


D, T, I, Q = 512, 1024, 512, 128


def setup_inputs():
    n = np.random.standard_normal
    idx = np.stack([np.random.permutation(T)[:I] for _ in range(8)])
    idx2 = np.stack([np.random.permutation(T)[:I] for _ in range(8)])
    fd = mx_kscale(D)
    keysp = pack_weight(n((D, T)) / fd[:, None], "e4m3")
    return {
        "query": (n((D, Q)) * 0.9 / np.sqrt(D) * fd[:, None]).astype(np.float32),
        "query2": (n((D, Q)) * 0.9 / np.sqrt(D) * fd[:, None]).astype(np.float32),
        "keys_words": keysp[0],
        "keys_scales": keysp[1],
        "lam": (np.random.uniform(0.5, 1.5, (Q, 1))).astype(np.float32),
        "earlier": (np.random.uniform(0.1, 2.0, (Q, I))).astype(np.float32),
        "trust": (np.random.uniform(0.3, 0.8, (Q, 1))).astype(np.float32),
        "base": (0.3 * n((Q, I))).astype(np.float32),
        "gain2": (np.random.uniform(0.5, 2.0, (Q, 1))).astype(np.float32),
        "offs": striped8(idx),
        "offs2": striped8(idx2),
    }


def reference(query, query2, keys_words, keys_scales, lam, earlier, trust, base, gain2, offs, offs2):
    idx = unstriped8(offs)
    idx2 = unstriped8(offs2)
    keysu = unpack_weight(keys_words, keys_scales, "e4m3")
    queryq = mxq(f64(query), 0, "e4m3")
    a = queryq.T @ keysu
    query2q = mxq(f64(query2), 0, "e4m3")
    b = query2q.T @ keysu
    s = pick8(a, idx, 16) + pick8(a, idx2, 16) * np.tanh(pick8(b, idx, 16)) * f64(lam)
    p = np.exp(s - np.max(s, axis=1, keepdims=True))
    r = p / np.sum(p, axis=1, keepdims=True)
    re0 = f64(earlier) / np.sum(f64(earlier), axis=1, keepdims=True)
    w = r * f64(trust) + re0 * (1.0 - f64(trust))
    y = np.tanh(w * f64(gain2) * 256.0) + f64(base)
    return y

@@ -1,0 +1,172 @@
+from contextlib import ExitStack
+
+import concourse.mybir as mybir
+
+D, T, I, Q = 512, 1024, 512, 128
+FLOPS = 2 * 2 * D * T * Q
+
+F32 = mybir.dt.float32
+BF16 = mybir.dt.bfloat16
+I32 = mybir.dt.int32
+U32 = mybir.dt.uint32
+U16 = mybir.dt.uint16
+U8 = mybir.dt.uint8
+FP8X4 = mybir.dt.float8_e4m3fn_x4
+ALU = mybir.AluOpType
+ACT = mybir.ActivationFunctionType
+AX = mybir.AxisListType
+
+P = 128
+PACK = 4
+HALF_T = T // 2
+HALF_I = I // 2
+LIST_COLS = I // 16
+
+
+def tile_attend_turnedby_carried_gated_heads_kernel(
+    tc, query, query2, keys_words, keys_scales, lam, earlier, trust, base, gain2, offs, offs2, out
+):
+    nc = tc.nc
+    with ExitStack() as ctx:
+        sb = ctx.enter_context(tc.tile_pool(name="sb", bufs=1))
+        psum = ctx.enter_context(tc.psum_pool(name="psum", bufs=1))
+
+        key_scale = sb.tile([P, T], U8, name="key_scale", align_bytes=64)
+        nc.vector.memset(key_scale[:].bitcast(I32), 0)
+
+        words = keys_words[0].rearrange("p n t -> p (n t)")
+        key_code = [sb.tile([P, HALF_T], U32, name=f"key_code{h}", align_bytes=64) for h in range(2)]
+        raw_b = sb.tile([P, PACK, Q], F32, name="raw_b")
+        raw_a = sb.tile([P, PACK, Q], F32, name="raw_a")
+
+        def load_keys(h):
+            nc.sync.dma_start(
+                out=key_code[h][:].bitcast(I32),
+                in_=words[:, h * HALF_T * PACK : (h + 1) * HALF_T * PACK].bitcast(I32),
+            )
+
+        nc.sync.dma_start(out=raw_b[:], in_=query2.rearrange("(p j) q -> p j q", j=PACK))
+        for quad in range(4):
+            nc.sync.dma_start(
+                out=key_scale[32 * quad : 32 * quad + 4, :].bitcast(I32),
+                in_=keys_scales[0][4 * quad : 4 * quad + 4, :].bitcast(I32),
+            )
+        load_keys(0)
+        nc.sync.dma_start(out=raw_a[:], in_=query.rearrange("(p j) q -> p j q", j=PACK))
+        load_keys(1)
+
+        idx = sb.tile([P, LIST_COLS], U16, name="idx")
+        idx2 = sb.tile([P, LIST_COLS], U16, name="idx2")
+        nc.sync.dma_start(idx[:], offs)
+        nc.sync.dma_start(idx2[:], offs2)
+        earlier_sb = sb.tile([P, I], F32, name="earlier_sb")
+        base_sb = sb.tile([P, I], F32, name="base_sb")
+        nc.sync.dma_start(out=earlier_sb[:], in_=earlier)
+        nc.sync.dma_start(out=base_sb[:], in_=base)
+
+        lam_sb = sb.tile([P, 1], F32, name="lam_sb")
+        trust_sb = sb.tile([P, 1], F32, name="trust_sb")
+        gain_sb = sb.tile([P, 1], F32, name="gain_sb")
+        nc.gpsimd.dma_start(out=trust_sb[:], in_=trust)
+        nc.gpsimd.dma_start(out=gain_sb[:], in_=gain2)
+        nc.gpsimd.dma_start(out=lam_sb[:], in_=lam)
+
+        share_gain = sb.tile([P, 1], F32, name="share_gain")
+        distrust = sb.tile([P, 1], F32, name="distrust")
+        carry_gain = sb.tile([P, 1], F32, name="carry_gain")
+        nc.gpsimd.tensor_scalar(share_gain[:], trust_sb[:], gain_sb[:], 256.0, ALU.mult, ALU.mult)
+        nc.gpsimd.tensor_scalar(distrust[:], trust_sb[:], -1.0, 1.0, ALU.mult, ALU.add)
+        nc.gpsimd.tensor_scalar(carry_gain[:], distrust[:], gain_sb[:], 256.0, ALU.mult, ALU.mult)
+
+        def quantise(raw, tag):
+            grouped = sb.tile([P, Q, PACK], BF16, name=f"grouped_{tag}", align_bytes=64)
+            code = sb.tile([P, Q], U32, name=f"code_{tag}", align_bytes=64)
+            scale = sb.tile([P, Q], U8, name=f"scale_{tag}", align_bytes=64)
+            nc.vector.tensor_copy(out=grouped[:], in_=raw[:].rearrange("p j q -> p q j"))
+            nc.vector.quantize_mx(
+                out=code[:].bitcast(FP8X4), scales=scale[:], in_=grouped[:].rearrange("p q j -> p (q j)")
+            )
+            return code, scale
+
+        def score(operand, start, width, tag):
+            code, scale = operand
+            bank = psum.tile([P, width], F32, name=f"bank_{tag}")
+            h, local = divmod(start, HALF_T)
+            nc.tensor.matmul_mx(
+                out=bank[:],
+                lhsT=code[:].bitcast(FP8X4),
+                lhsT_scale=scale[:],
+                rhs=key_code[h][:, local : local + width].bitcast(FP8X4),
+                rhs_scale=key_scale[:, start : start + width],
+                start=True,
+                stop=True,
+            )
+            return bank
+
+        a_sb = sb.tile([P, T], F32, name="a_sb")
+        b_sb = sb.tile([P, T], F32, name="b_sb")
+
+        qb = quantise(raw_b, "b")
+        bank = score(qb, 0, 512, "b0")
+        nc.scalar.activation(b_sb[:, 0:512], bank[:], ACT.Copy)
+        qa = quantise(raw_a, "a")
+        bank = score(qb, 512, 256, "b1")
+        nc.scalar.activation(b_sb[:, 512:768], bank[:], ACT.Copy)
+        bank = score(qb, 768, 256, "b2")
+        nc.vector.tensor_copy(out=b_sb[:, 768:1024], in_=bank[:])
+        for c in range(4):
+            bank = score(qa, 256 * c, 256, f"a{c}")
+            nc.vector.tensor_copy(out=a_sb[:, 256 * c : 256 * (c + 1)], in_=bank[:])
+
+        halves = [slice(h * HALF_I, (h + 1) * HALF_I) for h in range(2)]
+        cols = [slice(h * LIST_COLS // 2, (h + 1) * LIST_COLS // 2) for h in range(2)]
+        b_pick = sb.tile([P, I], F32, name="b_pick")
+        gate = sb.tile([P, I], F32, name="gate")
+        a_pick = sb.tile([P, I], F32, name="a_pick")
+        turned = sb.tile([P, I], F32, name="turned")
+        s = sb.tile([P, I], F32, name="s")
+        for h in range(2):
+            nc.scalar.activation(b_pick[:, halves[h]], b_sb[:].indirect(idx[:, cols[h]]), ACT.Copy)
+            nc.scalar.activation(gate[:, halves[h]], b_pick[:, halves[h]], ACT.Tanh)
+        for h in range(2):
+            nc.vector.tensor_tensor(
+                turned[:, halves[h]], a_sb[:].indirect(idx2[:, cols[h]]), gate[:, halves[h]], ALU.mult
+            )
+            nc.scalar.activation(a_pick[:, halves[h]], a_sb[:].indirect(idx[:, cols[h]]), ACT.Copy)
+        for h in range(2):
+            nc.vector.scalar_tensor_tensor(
+                s[:, halves[h]], turned[:, halves[h]], lam_sb[:], a_pick[:, halves[h]], ALU.mult, ALU.add
+            )
+        neg_max = sb.tile([P, 1], F32, name="neg_max")
+        nc.vector.tensor_reduce(neg_max[:], s[:], AX.X, ALU.max, negate=True)
+
+        earlier_sum = sb.tile([P, 1], F32, name="earlier_sum")
+        earlier_copy = sb.tile([P, I], F32, name="earlier_copy")
+        nc.scalar.activation(earlier_copy[:], earlier_sb[:], ACT.Copy, accum_out=earlier_sum[:])
+
+        p = sb.tile([P, I], F32, name="p")
+        p_sum = sb.tile([P, 1], F32, name="p_sum")
+        nc.scalar.activation(p[:], s[:], ACT.Exp, bias=neg_max[:], accum_out=p_sum[:])
+
+        earlier_inv = sb.tile([P, 1], F32, name="earlier_inv")
+        carried = sb.tile([P, I], F32, name="carried")
+        nc.vector.reciprocal(earlier_inv[:], earlier_sum[:])
+        nc.vector.tensor_scalar(carried[:], earlier_copy[:], earlier_inv[:], carry_gain[:], ALU.mult, ALU.mult)
+
+        p_inv = sb.tile([P, 1], F32, name="p_inv")
+        p_gain = sb.tile([P, 1], F32, name="p_gain")
+        nc.vector.reciprocal(p_inv[:], p_sum[:])
+        nc.vector.tensor_tensor(p_gain[:], p_inv[:], share_gain[:], ALU.mult)
+
+        z = sb.tile([P, I], F32, name="z")
+        y = sb.tile([P, I], F32, name="y")
+        res = sb.tile([P, I], F32, name="res")
+        parts = [slice(128 * c, 128 * (c + 1)) for c in range(4)]
+        for c in range(4):
+            nc.vector.scalar_tensor_tensor(
+                z[:, parts[c]], p[:, parts[c]], p_gain[:], carried[:, parts[c]], ALU.mult, ALU.add
+            )
+            nc.scalar.activation(y[:, parts[c]], z[:, parts[c]], ACT.Tanh)
+        for h in range(2):
+            nc.vector.tensor_tensor(res[:, halves[h]], y[:, halves[h]], base_sb[:, halves[h]], ALU.add)
+            nc.sync.dma_start(out=out[:, halves[h]], in_=res[:, halves[h]])

@@ -18,7 +18,7 @@ AX = mybir.AxisListType
 
 P = 128
 PACK = 4
-HALF_T = T // 2
+FIRST_T = 768
 HALF_I = I // 2
 LIST_COLS = I // 16
 
@@ -35,23 +35,24 @@ def tile_attend_turnedby_carried_gated_heads_kernel(
         nc.vector.memset(key_scale[:].bitcast(I32), 0)
 
         words = keys_words[0].rearrange("p n t -> p (n t)")
-        key_code = [sb.tile([P, HALF_T], U32, name=f"key_code{h}", align_bytes=64) for h in range(2)]
+        spans = [(0, FIRST_T), (FIRST_T, T)]
+        key_code = [sb.tile([P, e - b], U32, name=f"key_code{b}", align_bytes=64) for b, e in spans]
         raw_b = sb.tile([P, PACK, Q], F32, name="raw_b")
         raw_a = sb.tile([P, PACK, Q], F32, name="raw_a")
 
         def load_keys(h):
             nc.sync.dma_start(
                 out=key_code[h][:].bitcast(I32),
-                in_=words[:, h * HALF_T * PACK : (h + 1) * HALF_T * PACK].bitcast(I32),
+                in_=words[:, spans[h][0] * PACK : spans[h][1] * PACK].bitcast(I32),
             )
 
         nc.sync.dma_start(out=raw_b[:], in_=query2.rearrange("(p j) q -> p j q", j=PACK))
+        load_keys(0)
         for quad in range(4):
             nc.sync.dma_start(
                 out=key_scale[32 * quad : 32 * quad + 4, :].bitcast(I32),
                 in_=keys_scales[0][4 * quad : 4 * quad + 4, :].bitcast(I32),
             )
-        load_keys(0)
         nc.sync.dma_start(out=raw_a[:], in_=query.rearrange("(p j) q -> p j q", j=PACK))
         load_keys(1)
 
@@ -61,37 +62,34 @@ def tile_attend_turnedby_carried_gated_heads_kernel(
         nc.sync.dma_start(idx2[:], offs2)
         earlier_sb = sb.tile([P, I], F32, name="earlier_sb")
         base_sb = sb.tile([P, I], F32, name="base_sb")
-        nc.sync.dma_start(out=earlier_sb[:], in_=earlier)
-        nc.sync.dma_start(out=base_sb[:], in_=base)
-
         lam_sb = sb.tile([P, 1], F32, name="lam_sb")
         trust_sb = sb.tile([P, 1], F32, name="trust_sb")
         gain_sb = sb.tile([P, 1], F32, name="gain_sb")
-        nc.gpsimd.dma_start(out=trust_sb[:], in_=trust)
-        nc.gpsimd.dma_start(out=gain_sb[:], in_=gain2)
-        nc.gpsimd.dma_start(out=lam_sb[:], in_=lam)
-
-        share_gain = sb.tile([P, 1], F32, name="share_gain")
-        distrust = sb.tile([P, 1], F32, name="distrust")
-        carry_gain = sb.tile([P, 1], F32, name="carry_gain")
-        nc.gpsimd.tensor_scalar(share_gain[:], trust_sb[:], gain_sb[:], 256.0, ALU.mult, ALU.mult)
-        nc.gpsimd.tensor_scalar(distrust[:], trust_sb[:], -1.0, 1.0, ALU.mult, ALU.add)
-        nc.gpsimd.tensor_scalar(carry_gain[:], distrust[:], gain_sb[:], 256.0, ALU.mult, ALU.mult)
+        nc.sync.dma_start(out=earlier_sb[:], in_=earlier)
+        nc.sync.dma_start(out=lam_sb[:], in_=lam)
+        nc.sync.dma_start(out=trust_sb[:], in_=trust)
+        nc.sync.dma_start(out=gain_sb[:], in_=gain2)
+        nc.sync.dma_start(out=base_sb[:], in_=base)
 
         def quantise(raw, tag):
             grouped = sb.tile([P, Q, PACK], BF16, name=f"grouped_{tag}", align_bytes=64)
             code = sb.tile([P, Q], U32, name=f"code_{tag}", align_bytes=64)
             scale = sb.tile([P, Q], U8, name=f"scale_{tag}", align_bytes=64)
-            nc.vector.tensor_copy(out=grouped[:], in_=raw[:].rearrange("p j q -> p q j"))
-            nc.vector.quantize_mx(
-                out=code[:].bitcast(FP8X4), scales=scale[:], in_=grouped[:].rearrange("p q j -> p (q j)")
-            )
+            rows = [slice(0, Q // 2), slice(Q // 2, Q)]
+            for r in rows:
+                nc.vector.tensor_copy(out=grouped[:, r, :], in_=raw[:, :, r].rearrange("p j q -> p q j"))
+            for r in rows:
+                nc.vector.quantize_mx(
+                    out=code[:, r].bitcast(FP8X4),
+                    scales=scale[:, r],
+                    in_=grouped[:, r, :].rearrange("p q j -> p (q j)"),
+                )
             return code, scale
 
         def score(operand, start, width, tag):
             code, scale = operand
             bank = psum.tile([P, width], F32, name=f"bank_{tag}")
-            h, local = divmod(start, HALF_T)
+            h, local = divmod(start, FIRST_T)
             nc.tensor.matmul_mx(
                 out=bank[:],
                 lhsT=code[:].bitcast(FP8X4),
@@ -107,32 +105,30 @@ def tile_attend_turnedby_carried_gated_heads_kernel(
         b_sb = sb.tile([P, T], F32, name="b_sb")
 
         qb = quantise(raw_b, "b")
-        bank = score(qb, 0, 512, "b0")
-        nc.scalar.activation(b_sb[:, 0:512], bank[:], ACT.Copy)
         qa = quantise(raw_a, "a")
-        bank = score(qb, 512, 256, "b1")
-        nc.scalar.activation(b_sb[:, 512:768], bank[:], ACT.Copy)
-        bank = score(qb, 768, 256, "b2")
-        nc.vector.tensor_copy(out=b_sb[:, 768:1024], in_=bank[:])
-        for c in range(4):
-            bank = score(qa, 256 * c, 256, f"a{c}")
-            nc.vector.tensor_copy(out=a_sb[:, 256 * c : 256 * (c + 1)], in_=bank[:])
+        for operand, dest, tag in ((qb, b_sb, "b"), (qa, a_sb, "a")):
+            for c in range(4):
+                bank = score(operand, 256 * c, 256, f"{tag}{c}")
+                nc.scalar.activation(dest[:, 256 * c : 256 * (c + 1)], bank[:], ACT.Copy)
 
         halves = [slice(h * HALF_I, (h + 1) * HALF_I) for h in range(2)]
         cols = [slice(h * LIST_COLS // 2, (h + 1) * LIST_COLS // 2) for h in range(2)]
-        b_pick = sb.tile([P, I], F32, name="b_pick")
+        s = sb.tile([P, I], F32, name="s")
         gate = sb.tile([P, I], F32, name="gate")
         a_pick = sb.tile([P, I], F32, name="a_pick")
+        a2_pick = sb.tile([P, HALF_I], F32, name="a2_pick")
         turned = sb.tile([P, I], F32, name="turned")
-        s = sb.tile([P, I], F32, name="s")
+        lo, hi = halves
+        b_pick = [s[:, hi], s[:, lo]]
         for h in range(2):
-            nc.scalar.activation(b_pick[:, halves[h]], b_sb[:].indirect(idx[:, cols[h]]), ACT.Copy)
-            nc.scalar.activation(gate[:, halves[h]], b_pick[:, halves[h]], ACT.Tanh)
-        for h in range(2):
-            nc.vector.tensor_tensor(
-                turned[:, halves[h]], a_sb[:].indirect(idx2[:, cols[h]]), gate[:, halves[h]], ALU.mult
-            )
-            nc.scalar.activation(a_pick[:, halves[h]], a_sb[:].indirect(idx[:, cols[h]]), ACT.Copy)
+            nc.vector.tensor_copy(b_pick[h], b_sb[:].indirect(idx[:, cols[h]]))
+        nc.scalar.activation(gate[:, lo], b_pick[0], ACT.Tanh)
+        nc.scalar.activation(a2_pick[:], a_sb[:].indirect(idx2[:, cols[1]]), ACT.Copy)
+        nc.scalar.activation(gate[:, hi], b_pick[1], ACT.Tanh)
+        nc.scalar.activation(a_pick[:, hi], a_sb[:].indirect(idx[:, cols[1]]), ACT.Copy)
+        nc.vector.tensor_copy(a_pick[:, lo], a_sb[:].indirect(idx[:, cols[0]]))
+        nc.vector.tensor_tensor(turned[:, lo], a_sb[:].indirect(idx2[:, cols[0]]), gate[:, lo], ALU.mult)
+        nc.vector.tensor_tensor(turned[:, hi], a2_pick[:], gate[:, hi], ALU.mult)
         for h in range(2):
             nc.vector.scalar_tensor_tensor(
                 s[:, halves[h]], turned[:, halves[h]], lam_sb[:], a_pick[:, halves[h]], ALU.mult, ALU.add
@@ -141,7 +137,9 @@ def tile_attend_turnedby_carried_gated_heads_kernel(
         nc.vector.tensor_reduce(neg_max[:], s[:], AX.X, ALU.max, negate=True)
 
         earlier_sum = sb.tile([P, 1], F32, name="earlier_sum")
-        earlier_copy = sb.tile([P, I], F32, name="earlier_copy")
+        earlier_copy = a_pick
+        carry = sb.tile([P, 1], F32, name="carry")
+        nc.scalar.activation(carry[:], trust_sb[:], ACT.Copy, bias=256.0, scale=-256.0)
         nc.scalar.activation(earlier_copy[:], earlier_sb[:], ACT.Copy, accum_out=earlier_sum[:])
 
         p = sb.tile([P, I], F32, name="p")
@@ -151,12 +149,13 @@ def tile_attend_turnedby_carried_gated_heads_kernel(
         earlier_inv = sb.tile([P, 1], F32, name="earlier_inv")
         carried = sb.tile([P, I], F32, name="carried")
         nc.vector.reciprocal(earlier_inv[:], earlier_sum[:])
-        nc.vector.tensor_scalar(carried[:], earlier_copy[:], earlier_inv[:], carry_gain[:], ALU.mult, ALU.mult)
+        nc.vector.tensor_scalar(carried[:], earlier_copy[:], earlier_inv[:], carry[:], ALU.mult, ALU.mult)
 
         p_inv = sb.tile([P, 1], F32, name="p_inv")
-        p_gain = sb.tile([P, 1], F32, name="p_gain")
+        trusted = sb.tile([P, I], F32, name="trusted")
         nc.vector.reciprocal(p_inv[:], p_sum[:])
-        nc.vector.tensor_tensor(p_gain[:], p_inv[:], share_gain[:], ALU.mult)
+        for h in range(2):
+            nc.vector.tensor_scalar(trusted[:, halves[h]], p[:, halves[h]], trust_sb[:], 256.0, ALU.mult, ALU.mult)
 
         z = sb.tile([P, I], F32, name="z")
         y = sb.tile([P, I], F32, name="y")
@@ -164,9 +163,12 @@ def tile_attend_turnedby_carried_gated_heads_kernel(
         parts = [slice(128 * c, 128 * (c + 1)) for c in range(4)]
         for c in range(4):
             nc.vector.scalar_tensor_tensor(
-                z[:, parts[c]], p[:, parts[c]], p_gain[:], carried[:, parts[c]], ALU.mult, ALU.add
+                z[:, parts[c]], trusted[:, parts[c]], p_inv[:], carried[:, parts[c]], ALU.mult, ALU.add
             )
-            nc.scalar.activation(y[:, parts[c]], z[:, parts[c]], ACT.Tanh)
-        for h in range(2):
-            nc.vector.tensor_tensor(res[:, halves[h]], y[:, halves[h]], base_sb[:, halves[h]], ALU.add)
-            nc.sync.dma_start(out=out[:, halves[h]], in_=res[:, halves[h]])
+            nc.scalar.activation(y[:, parts[c]], z[:, parts[c]], ACT.Tanh, scale=gain_sb[:])
+        stores = {1: (slice(0, 256), nc.sync), 2: (parts[2], nc.scalar), 3: (parts[3], nc.sync)}
+        for c in range(4):
+            nc.vector.tensor_tensor(res[:, parts[c]], y[:, parts[c]], base_sb[:, parts[c]], ALU.add)
+            if c in stores:
+                piece, queue = stores[c]
+                queue.dma_start(out=out[:, piece], in_=res[:, piece])

@@ -137,19 +137,19 @@ def tile_attend_turnedby_carried_gated_heads_kernel(
         nc.vector.tensor_reduce(neg_max[:], s[:], AX.X, ALU.max, negate=True)
 
         earlier_sum = sb.tile([P, 1], F32, name="earlier_sum")
-        earlier_copy = a_pick
-        carry = sb.tile([P, 1], F32, name="carry")
-        nc.scalar.activation(carry[:], trust_sb[:], ACT.Copy, bias=256.0, scale=-256.0)
+        earlier_copy = gate
+        carry = a2_pick[:, 0:1]
+        nc.scalar.activation(carry, trust_sb[:], ACT.Copy, bias=256.0, scale=-256.0)
         nc.scalar.activation(earlier_copy[:], earlier_sb[:], ACT.Copy, accum_out=earlier_sum[:])
 
         p = sb.tile([P, I], F32, name="p")
         p_sum = sb.tile([P, 1], F32, name="p_sum")
         nc.scalar.activation(p[:], s[:], ACT.Exp, bias=neg_max[:], accum_out=p_sum[:])
 
-        earlier_inv = sb.tile([P, 1], F32, name="earlier_inv")
+        earlier_inv = turned[:, I - 1 : I]
         carried = sb.tile([P, I], F32, name="carried")
-        nc.vector.reciprocal(earlier_inv[:], earlier_sum[:])
-        nc.vector.tensor_scalar(carried[:], earlier_copy[:], earlier_inv[:], carry[:], ALU.mult, ALU.mult)
+        nc.vector.reciprocal(earlier_inv, earlier_sum[:])
+        nc.vector.tensor_scalar(carried[:], earlier_copy[:], earlier_inv, carry, ALU.mult, ALU.mult)
 
         p_inv = sb.tile([P, 1], F32, name="p_inv")
         trusted = sb.tile([P, I], F32, name="trusted")
@@ -166,9 +166,7 @@ def tile_attend_turnedby_carried_gated_heads_kernel(
                 z[:, parts[c]], trusted[:, parts[c]], p_inv[:], carried[:, parts[c]], ALU.mult, ALU.add
             )
             nc.scalar.activation(y[:, parts[c]], z[:, parts[c]], ACT.Tanh, scale=gain_sb[:])
-        stores = {1: (slice(0, 256), nc.sync), 2: (parts[2], nc.scalar), 3: (parts[3], nc.sync)}
         for c in range(4):
             nc.vector.tensor_tensor(res[:, parts[c]], y[:, parts[c]], base_sb[:, parts[c]], ALU.add)
-            if c in stores:
-                piece, queue = stores[c]
-                queue.dma_start(out=out[:, piece], in_=res[:, piece])
+            if c % 2 == 1:
+                nc.sync.dma_start(out=out[:, halves[c // 2]], in_=res[:, halves[c // 2]])

@@ -18,9 +18,16 @@ AX = mybir.AxisListType
 
 P = 128
 PACK = 4
-FIRST_T = 768
+QUADRANT = 32
+SCALE_ROWS = 4
+CHUNK = 256
+CHUNKS = T // CHUNK
+FIRST_T = 3 * CHUNK
 HALF_I = I // 2
 LIST_COLS = I // 16
+PART = 128
+PARTS = I // PART
+OUT_SCALE = 256.0
 
 
 def tile_attend_turnedby_carried_gated_heads_kernel(
@@ -31,27 +38,28 @@ def tile_attend_turnedby_carried_gated_heads_kernel(
         sb = ctx.enter_context(tc.tile_pool(name="sb", bufs=1))
         psum = ctx.enter_context(tc.psum_pool(name="psum", bufs=1))
 
-        key_scale = sb.tile([P, T], U8, name="key_scale", align_bytes=64)
+        key_scale = sb.tile([P, CHUNK], U8, name="key_scale", align_bytes=64)
         nc.vector.memset(key_scale[:].bitcast(I32), 0)
 
         words = keys_words[0].rearrange("p n t -> p (n t)")
         spans = [(0, FIRST_T), (FIRST_T, T)]
-        key_code = [sb.tile([P, e - b], U32, name=f"key_code{b}", align_bytes=64) for b, e in spans]
+        key_code = [sb.tile([P, end - begin], U32, name=f"key_code{begin}", align_bytes=64) for begin, end in spans]
         raw_b = sb.tile([P, PACK, Q], F32, name="raw_b")
         raw_a = sb.tile([P, PACK, Q], F32, name="raw_a")
 
-        def load_keys(h):
+        def load_keys(span):
+            begin, end = spans[span]
             nc.sync.dma_start(
-                out=key_code[h][:].bitcast(I32),
-                in_=words[:, spans[h][0] * PACK : spans[h][1] * PACK].bitcast(I32),
+                out=key_code[span][:].bitcast(I32), in_=words[:, begin * PACK : end * PACK].bitcast(I32)
             )
 
         nc.sync.dma_start(out=raw_b[:], in_=query2.rearrange("(p j) q -> p j q", j=PACK))
         load_keys(0)
-        for quad in range(4):
+        for quad in range(P // QUADRANT):
+            blocks = keys_scales[0][SCALE_ROWS * quad : SCALE_ROWS * (quad + 1), :].bitcast(I32)
             nc.sync.dma_start(
-                out=key_scale[32 * quad : 32 * quad + 4, :].bitcast(I32),
-                in_=keys_scales[0][4 * quad : 4 * quad + 4, :].bitcast(I32),
+                out=key_scale[QUADRANT * quad : QUADRANT * quad + SCALE_ROWS * CHUNKS, :].bitcast(I32),
+                in_=blocks.rearrange("r (c n) -> c r n", c=CHUNKS),
             )
         nc.sync.dma_start(out=raw_a[:], in_=query.rearrange("(p j) q -> p j q", j=PACK))
         load_keys(1)
@@ -75,27 +83,27 @@ def tile_attend_turnedby_carried_gated_heads_kernel(
             grouped = sb.tile([P, Q, PACK], BF16, name=f"grouped_{tag}", align_bytes=64)
             code = sb.tile([P, Q], U32, name=f"code_{tag}", align_bytes=64)
             scale = sb.tile([P, Q], U8, name=f"scale_{tag}", align_bytes=64)
-            rows = [slice(0, Q // 2), slice(Q // 2, Q)]
-            for r in rows:
-                nc.vector.tensor_copy(out=grouped[:, r, :], in_=raw[:, :, r].rearrange("p j q -> p q j"))
-            for r in rows:
+            row_halves = [slice(0, Q // 2), slice(Q // 2, Q)]
+            for rows in row_halves:
+                nc.vector.tensor_copy(out=grouped[:, rows, :], in_=raw[:, :, rows].rearrange("p j q -> p q j"))
+            for rows in row_halves:
                 nc.vector.quantize_mx(
-                    out=code[:, r].bitcast(FP8X4),
-                    scales=scale[:, r],
-                    in_=grouped[:, r, :].rearrange("p q j -> p (q j)"),
+                    out=code[:, rows].bitcast(FP8X4),
+                    scales=scale[:, rows],
+                    in_=grouped[:, rows, :].rearrange("p q j -> p (q j)"),
                 )
             return code, scale
 
-        def score(operand, start, width, tag):
+        def score(operand, chunk, tag):
             code, scale = operand
-            bank = psum.tile([P, width], F32, name=f"bank_{tag}")
-            h, local = divmod(start, FIRST_T)
+            bank = psum.tile([P, CHUNK], F32, name=f"bank_{tag}{chunk}")
+            span, local = divmod(chunk * CHUNK, FIRST_T)
             nc.tensor.matmul_mx(
                 out=bank[:],
                 lhsT=code[:].bitcast(FP8X4),
                 lhsT_scale=scale[:],
-                rhs=key_code[h][:, local : local + width].bitcast(FP8X4),
-                rhs_scale=key_scale[:, start : start + width],
+                rhs=key_code[span][:, local : local + CHUNK].bitcast(FP8X4),
+                rhs_scale=key_scale[SCALE_ROWS * chunk :, :],
                 start=True,
                 stop=True,
             )
@@ -104,42 +112,43 @@ def tile_attend_turnedby_carried_gated_heads_kernel(
         a_sb = sb.tile([P, T], F32, name="a_sb")
         b_sb = sb.tile([P, T], F32, name="b_sb")
 
-        qb = quantise(raw_b, "b")
-        qa = quantise(raw_a, "a")
-        for operand, dest, tag in ((qb, b_sb, "b"), (qa, a_sb, "a")):
-            for c in range(4):
-                bank = score(operand, 256 * c, 256, f"{tag}{c}")
-                nc.scalar.activation(dest[:, 256 * c : 256 * (c + 1)], bank[:], ACT.Copy)
+        quantised_b = quantise(raw_b, "b")
+        quantised_a = quantise(raw_a, "a")
+        for operand, window, tag in ((quantised_b, b_sb, "b"), (quantised_a, a_sb, "a")):
+            for chunk in range(CHUNKS):
+                bank = score(operand, chunk, tag)
+                nc.scalar.activation(window[:, CHUNK * chunk : CHUNK * (chunk + 1)], bank[:], ACT.Copy)
 
         halves = [slice(h * HALF_I, (h + 1) * HALF_I) for h in range(2)]
-        cols = [slice(h * LIST_COLS // 2, (h + 1) * LIST_COLS // 2) for h in range(2)]
+        list_halves = [slice(h * LIST_COLS // 2, (h + 1) * LIST_COLS // 2) for h in range(2)]
         s = sb.tile([P, I], F32, name="s")
         gate = sb.tile([P, I], F32, name="gate")
         a_pick = sb.tile([P, I], F32, name="a_pick")
         a2_pick = sb.tile([P, HALF_I], F32, name="a2_pick")
         turned = sb.tile([P, I], F32, name="turned")
         lo, hi = halves
+
         b_pick = [s[:, hi], s[:, lo]]
         for h in range(2):
-            nc.vector.tensor_copy(b_pick[h], b_sb[:].indirect(idx[:, cols[h]]))
+            nc.vector.tensor_copy(b_pick[h], b_sb[:].indirect(idx[:, list_halves[h]]))
         nc.scalar.activation(gate[:, lo], b_pick[0], ACT.Tanh)
-        nc.scalar.activation(a2_pick[:], a_sb[:].indirect(idx2[:, cols[1]]), ACT.Copy)
+        nc.scalar.activation(a2_pick[:], a_sb[:].indirect(idx2[:, list_halves[1]]), ACT.Copy)
         nc.scalar.activation(gate[:, hi], b_pick[1], ACT.Tanh)
-        nc.scalar.activation(a_pick[:, hi], a_sb[:].indirect(idx[:, cols[1]]), ACT.Copy)
-        nc.vector.tensor_copy(a_pick[:, lo], a_sb[:].indirect(idx[:, cols[0]]))
-        nc.vector.tensor_tensor(turned[:, lo], a_sb[:].indirect(idx2[:, cols[0]]), gate[:, lo], ALU.mult)
+        nc.scalar.activation(a_pick[:, hi], a_sb[:].indirect(idx[:, list_halves[1]]), ACT.Copy)
+        nc.vector.tensor_copy(a_pick[:, lo], a_sb[:].indirect(idx[:, list_halves[0]]))
+        nc.vector.tensor_tensor(turned[:, lo], a_sb[:].indirect(idx2[:, list_halves[0]]), gate[:, lo], ALU.mult)
         nc.vector.tensor_tensor(turned[:, hi], a2_pick[:], gate[:, hi], ALU.mult)
-        for h in range(2):
+        for half in halves:
             nc.vector.scalar_tensor_tensor(
-                s[:, halves[h]], turned[:, halves[h]], lam_sb[:], a_pick[:, halves[h]], ALU.mult, ALU.add
+                s[:, half], turned[:, half], lam_sb[:], a_pick[:, half], ALU.mult, ALU.add
             )
         neg_max = sb.tile([P, 1], F32, name="neg_max")
         nc.vector.tensor_reduce(neg_max[:], s[:], AX.X, ALU.max, negate=True)
 
         earlier_sum = sb.tile([P, 1], F32, name="earlier_sum")
         earlier_copy = gate
-        carry = a2_pick[:, 0:1]
-        nc.scalar.activation(carry, trust_sb[:], ACT.Copy, bias=256.0, scale=-256.0)
+        distrust = a2_pick[:, 0:1]
+        nc.scalar.activation(distrust, trust_sb[:], ACT.Copy, bias=OUT_SCALE, scale=-OUT_SCALE)
         nc.scalar.activation(earlier_copy[:], earlier_sb[:], ACT.Copy, accum_out=earlier_sum[:])
 
         p = sb.tile([P, I], F32, name="p")
@@ -149,24 +158,24 @@ def tile_attend_turnedby_carried_gated_heads_kernel(
         earlier_inv = turned[:, I - 1 : I]
         carried = sb.tile([P, I], F32, name="carried")
         nc.vector.reciprocal(earlier_inv, earlier_sum[:])
-        nc.vector.tensor_scalar(carried[:], earlier_copy[:], earlier_inv, carry, ALU.mult, ALU.mult)
+        nc.vector.tensor_scalar(carried[:], earlier_copy[:], earlier_inv, distrust, ALU.mult, ALU.mult)
 
         p_inv = sb.tile([P, 1], F32, name="p_inv")
         trusted = sb.tile([P, I], F32, name="trusted")
         nc.vector.reciprocal(p_inv[:], p_sum[:])
-        for h in range(2):
-            nc.vector.tensor_scalar(trusted[:, halves[h]], p[:, halves[h]], trust_sb[:], 256.0, ALU.mult, ALU.mult)
+        for half in halves:
+            nc.vector.tensor_scalar(trusted[:, half], p[:, half], trust_sb[:], OUT_SCALE, ALU.mult, ALU.mult)
 
-        z = sb.tile([P, I], F32, name="z")
-        y = sb.tile([P, I], F32, name="y")
-        res = sb.tile([P, I], F32, name="res")
-        parts = [slice(128 * c, 128 * (c + 1)) for c in range(4)]
-        for c in range(4):
+        blend = sb.tile([P, I], F32, name="blend")
+        squashed = sb.tile([P, I], F32, name="squashed")
+        result = sb.tile([P, I], F32, name="result")
+        parts = [slice(PART * n, PART * (n + 1)) for n in range(PARTS)]
+        for part in parts:
             nc.vector.scalar_tensor_tensor(
-                z[:, parts[c]], trusted[:, parts[c]], p_inv[:], carried[:, parts[c]], ALU.mult, ALU.add
+                blend[:, part], trusted[:, part], p_inv[:], carried[:, part], ALU.mult, ALU.add
             )
-            nc.scalar.activation(y[:, parts[c]], z[:, parts[c]], ACT.Tanh, scale=gain_sb[:])
-        for c in range(4):
-            nc.vector.tensor_tensor(res[:, parts[c]], y[:, parts[c]], base_sb[:, parts[c]], ALU.add)
-            if c % 2 == 1:
-                nc.sync.dma_start(out=out[:, halves[c // 2]], in_=res[:, halves[c // 2]])
+            nc.scalar.activation(squashed[:, part], blend[:, part], ACT.Tanh, scale=gain_sb[:])
+        for h, half in enumerate(halves):
+            for part in parts[h * PARTS // 2 : (h + 1) * PARTS // 2]:
+                nc.vector.tensor_tensor(result[:, part], squashed[:, part], base_sb[:, part], ALU.add)
+            nc.sync.dma_start(out=out[:, half], in_=result[:, half])

from contextlib import ExitStack

import concourse.mybir as mybir

D, T, I, Q = 512, 1024, 512, 128
FLOPS = 2 * 2 * D * T * Q

F32 = mybir.dt.float32
BF16 = mybir.dt.bfloat16
I32 = mybir.dt.int32
U32 = mybir.dt.uint32
U16 = mybir.dt.uint16
U8 = mybir.dt.uint8
FP8X4 = mybir.dt.float8_e4m3fn_x4
ALU = mybir.AluOpType
ACT = mybir.ActivationFunctionType
AX = mybir.AxisListType

P = 128
PACK = 4
QUADRANT = 32
SCALE_ROWS = 4
CHUNK = 256
CHUNKS = T // CHUNK
FIRST_T = 3 * CHUNK
HALF_I = I // 2
LIST_COLS = I // 16
PART = 128
PARTS = I // PART
OUT_SCALE = 256.0


def tile_attend_turnedby_carried_gated_heads_kernel(
    tc, query, query2, keys_words, keys_scales, lam, earlier, trust, base, gain2, offs, offs2, out
):
    nc = tc.nc
    with ExitStack() as ctx:
        sb = ctx.enter_context(tc.tile_pool(name="sb", bufs=1))
        psum = ctx.enter_context(tc.psum_pool(name="psum", bufs=1))

        key_scale = sb.tile([P, CHUNK], U8, name="key_scale", align_bytes=64)
        nc.vector.memset(key_scale[:].bitcast(I32), 0)

        words = keys_words[0].rearrange("p n t -> p (n t)")
        spans = [(0, FIRST_T), (FIRST_T, T)]
        key_code = [sb.tile([P, end - begin], U32, name=f"key_code{begin}", align_bytes=64) for begin, end in spans]
        raw_b = sb.tile([P, PACK, Q], F32, name="raw_b")
        raw_a = sb.tile([P, PACK, Q], F32, name="raw_a")

        def load_keys(span):
            begin, end = spans[span]
            nc.sync.dma_start(
                out=key_code[span][:].bitcast(I32), in_=words[:, begin * PACK : end * PACK].bitcast(I32)
            )

        nc.sync.dma_start(out=raw_b[:], in_=query2.rearrange("(p j) q -> p j q", j=PACK))
        load_keys(0)
        for quad in range(P // QUADRANT):
            blocks = keys_scales[0][SCALE_ROWS * quad : SCALE_ROWS * (quad + 1), :].bitcast(I32)
            nc.sync.dma_start(
                out=key_scale[QUADRANT * quad : QUADRANT * quad + SCALE_ROWS * CHUNKS, :].bitcast(I32),
                in_=blocks.rearrange("r (c n) -> c r n", c=CHUNKS),
            )
        nc.sync.dma_start(out=raw_a[:], in_=query.rearrange("(p j) q -> p j q", j=PACK))
        load_keys(1)

        idx = sb.tile([P, LIST_COLS], U16, name="idx")
        idx2 = sb.tile([P, LIST_COLS], U16, name="idx2")
        nc.sync.dma_start(idx[:], offs)
        nc.sync.dma_start(idx2[:], offs2)
        earlier_sb = sb.tile([P, I], F32, name="earlier_sb")
        base_sb = sb.tile([P, I], F32, name="base_sb")
        lam_sb = sb.tile([P, 1], F32, name="lam_sb")
        trust_sb = sb.tile([P, 1], F32, name="trust_sb")
        gain_sb = sb.tile([P, 1], F32, name="gain_sb")
        nc.sync.dma_start(out=earlier_sb[:], in_=earlier)
        nc.sync.dma_start(out=lam_sb[:], in_=lam)
        nc.sync.dma_start(out=trust_sb[:], in_=trust)
        nc.sync.dma_start(out=gain_sb[:], in_=gain2)
        nc.sync.dma_start(out=base_sb[:], in_=base)

        def quantise(raw, tag):
            grouped = sb.tile([P, Q, PACK], BF16, name=f"grouped_{tag}", align_bytes=64)
            code = sb.tile([P, Q], U32, name=f"code_{tag}", align_bytes=64)
            scale = sb.tile([P, Q], U8, name=f"scale_{tag}", align_bytes=64)
            row_halves = [slice(0, Q // 2), slice(Q // 2, Q)]
            for rows in row_halves:
                nc.vector.tensor_copy(out=grouped[:, rows, :], in_=raw[:, :, rows].rearrange("p j q -> p q j"))
            for rows in row_halves:
                nc.vector.quantize_mx(
                    out=code[:, rows].bitcast(FP8X4),
                    scales=scale[:, rows],
                    in_=grouped[:, rows, :].rearrange("p q j -> p (q j)"),
                )
            return code, scale

        def score(operand, chunk, tag):
            code, scale = operand
            bank = psum.tile([P, CHUNK], F32, name=f"bank_{tag}{chunk}")
            span, local = divmod(chunk * CHUNK, FIRST_T)
            nc.tensor.matmul_mx(
                out=bank[:],
                lhsT=code[:].bitcast(FP8X4),
                lhsT_scale=scale[:],
                rhs=key_code[span][:, local : local + CHUNK].bitcast(FP8X4),
                rhs_scale=key_scale[SCALE_ROWS * chunk :, :],
                start=True,
                stop=True,
            )
            return bank

        a_sb = sb.tile([P, T], F32, name="a_sb")
        b_sb = sb.tile([P, T], F32, name="b_sb")

        quantised_b = quantise(raw_b, "b")
        quantised_a = quantise(raw_a, "a")
        for operand, window, tag in ((quantised_b, b_sb, "b"), (quantised_a, a_sb, "a")):
            for chunk in range(CHUNKS):
                bank = score(operand, chunk, tag)
                nc.scalar.activation(window[:, CHUNK * chunk : CHUNK * (chunk + 1)], bank[:], ACT.Copy)

        halves = [slice(h * HALF_I, (h + 1) * HALF_I) for h in range(2)]
        list_halves = [slice(h * LIST_COLS // 2, (h + 1) * LIST_COLS // 2) for h in range(2)]
        s = sb.tile([P, I], F32, name="s")
        gate = sb.tile([P, I], F32, name="gate")
        a_pick = sb.tile([P, I], F32, name="a_pick")
        a2_pick = sb.tile([P, HALF_I], F32, name="a2_pick")
        turned = sb.tile([P, I], F32, name="turned")
        lo, hi = halves

        b_pick = [s[:, hi], s[:, lo]]
        for h in range(2):
            nc.vector.tensor_copy(b_pick[h], b_sb[:].indirect(idx[:, list_halves[h]]))
        nc.scalar.activation(gate[:, lo], b_pick[0], ACT.Tanh)
        nc.scalar.activation(a2_pick[:], a_sb[:].indirect(idx2[:, list_halves[1]]), ACT.Copy)
        nc.scalar.activation(gate[:, hi], b_pick[1], ACT.Tanh)
        nc.scalar.activation(a_pick[:, hi], a_sb[:].indirect(idx[:, list_halves[1]]), ACT.Copy)
        nc.vector.tensor_copy(a_pick[:, lo], a_sb[:].indirect(idx[:, list_halves[0]]))
        nc.vector.tensor_tensor(turned[:, lo], a_sb[:].indirect(idx2[:, list_halves[0]]), gate[:, lo], ALU.mult)
        nc.vector.tensor_tensor(turned[:, hi], a2_pick[:], gate[:, hi], ALU.mult)
        for half in halves:
            nc.vector.scalar_tensor_tensor(
                s[:, half], turned[:, half], lam_sb[:], a_pick[:, half], ALU.mult, ALU.add
            )
        neg_max = sb.tile([P, 1], F32, name="neg_max")
        nc.vector.tensor_reduce(neg_max[:], s[:], AX.X, ALU.max, negate=True)

        earlier_sum = sb.tile([P, 1], F32, name="earlier_sum")
        earlier_copy = gate
        distrust = a2_pick[:, 0:1]
        nc.scalar.activation(distrust, trust_sb[:], ACT.Copy, bias=OUT_SCALE, scale=-OUT_SCALE)
        nc.scalar.activation(earlier_copy[:], earlier_sb[:], ACT.Copy, accum_out=earlier_sum[:])

        p = sb.tile([P, I], F32, name="p")
        p_sum = sb.tile([P, 1], F32, name="p_sum")
        nc.scalar.activation(p[:], s[:], ACT.Exp, bias=neg_max[:], accum_out=p_sum[:])

        earlier_inv = turned[:, I - 1 : I]
        carried = sb.tile([P, I], F32, name="carried")
        nc.vector.reciprocal(earlier_inv, earlier_sum[:])
        nc.vector.tensor_scalar(carried[:], earlier_copy[:], earlier_inv, distrust, ALU.mult, ALU.mult)

        p_inv = sb.tile([P, 1], F32, name="p_inv")
        trusted = sb.tile([P, I], F32, name="trusted")
        nc.vector.reciprocal(p_inv[:], p_sum[:])
        for half in halves:
            nc.vector.tensor_scalar(trusted[:, half], p[:, half], trust_sb[:], OUT_SCALE, ALU.mult, ALU.mult)

        blend = sb.tile([P, I], F32, name="blend")
        squashed = sb.tile([P, I], F32, name="squashed")
        result = sb.tile([P, I], F32, name="result")
        parts = [slice(PART * n, PART * (n + 1)) for n in range(PARTS)]
        for part in parts:
            nc.vector.scalar_tensor_tensor(
                blend[:, part], trusted[:, part], p_inv[:], carried[:, part], ALU.mult, ALU.add
            )
            nc.scalar.activation(squashed[:, part], blend[:, part], ACT.Tanh, scale=gain_sb[:])
        for h, half in enumerate(halves):
            for part in parts[h * PARTS // 2 : (h + 1) * PARTS // 2]:
                nc.vector.tensor_tensor(result[:, part], squashed[:, part], base_sb[:, part], ALU.add)
            nc.sync.dma_start(out=out[:, half], in_=result[:, half])
